import numpy as np
import ml_dtypes


def mxq(x, axis, fmt="e4m3"):
    dtype, down = {"e4m3": (ml_dtypes.float8_e4m3fn, 7), "e5m2": (ml_dtypes.float8_e5m2, 14)}[fmt]
    v = np.moveaxis(np.asarray(x, np.float32).astype(ml_dtypes.bfloat16).astype(np.float64), axis, -1)
    blocks = v.reshape(v.shape[:-1] + (-1, 32))
    amax = np.abs(blocks).max(-1, keepdims=True)
    byte = np.maximum(np.where(amax > 0, np.frexp(amax)[1] - 1 + 127, 0) - down, 1)
    scale = np.exp2(byte - 127.0)
    codes = (blocks / scale).astype(np.float32).astype(dtype).astype(np.float64)
    return np.moveaxis((codes * scale).reshape(v.shape), -1, axis)


WIDE = False


def mx_kscale(k):
    if not WIDE:
        return np.ones(k)
    levels = np.array([10, -10, 5, -5, 0])
    if k % 512:
        return np.exp2(np.random.permutation(np.resize(levels, k // 32))).repeat(32)
    a = np.empty((k // 512, 16))
    for p in range(k // 512):
        a[p, :8] = np.random.permutation(np.resize(levels, 8))
        for g in range(8):
            far = levels[np.abs(levels - a[p, g]) >= 10]
            a[p, g + 8] = far[np.random.randint(len(far))]
    return np.exp2(a.ravel()).repeat(32)


def f64(x):
    return np.asarray(x).astype(np.float64)


def striped(idx):
    return np.tile(idx.reshape(-1, 16).T, (8, 1)).astype(np.uint16)


def unstriped(offs):
    return offs[:16].T.reshape(-1).astype(np.int64)


E2M1 = np.array([0.0, 0.5, 1.0, 1.5, 2.0, 3.0, 4.0, 6.0, -0.0, -0.5, -1.0, -1.5, -2.0, -3.0, -4.0, -6.0])


def pack_weight(w, fmt):
    k, n = w.shape
    w = f64(np.asarray(w, np.float32).astype(ml_dtypes.bfloat16)).reshape(k // 32, 32, n)
    amax = np.abs(w).max(1)
    if fmt == "e4m3":
        byte = np.frexp(amax)[1] - 1 + 127 - 7
    else:
        mant, ex = np.frexp(amax / 6.0)
        byte = np.where(mant > 0.5, ex, ex - 1) + 127
    byte = np.clip(np.where(amax > 0, byte, 1), 1, 254)
    scaled = (w * np.exp2(127.0 - byte)[:, None, :]).reshape(k, n).astype(np.float32)
    by_word = np.ascontiguousarray(scaled.reshape(k // 512, 128, 4, n).transpose(0, 1, 3, 2))
    if fmt == "e4m3":
        words = by_word.astype(ml_dtypes.float8_e4m3fn).view(np.uint8)
    else:
        c = by_word.astype(ml_dtypes.float4_e2m1fn).view(np.uint8) & 0xF
        words = (c[..., 0::2] | (c[..., 1::2] << 4)).reshape(k // 512, 128, 2 * n)
    return np.ascontiguousarray(words), np.ascontiguousarray(byte.astype(np.uint8).reshape(k // 512, 16, n))


def unpack_weight(words, scales, fmt):
    g, _, n = scales.shape
    words = np.ascontiguousarray(words).reshape(g, 128, n, -1)
    if fmt == "e4m3":
        vals = words.view(ml_dtypes.float8_e4m3fn).astype(np.float64)
    else:
        nib = np.empty((g, 128, n, 4), np.uint8)
        nib[..., 0::2] = words & 0xF
        nib[..., 1::2] = words >> 4
        vals = E2M1[nib]
    vals = vals * np.repeat(np.exp2(scales.astype(np.float64) - 127.0), 8, axis=1)[..., None]
    return vals.transpose(0, 1, 3, 2).reshape(g * 512, n)


def gelu(v):
    return 0.5 * v * (1.0 + np.tanh(np.sqrt(2.0 / np.pi) * (v + 0.044715 * v**3)))


K, T, S, H, T2, P = 1024, 2048, 512, 1024, 1024, 512


def setup_inputs():
    n = np.random.standard_normal
    s = mx_kscale(K)[:, None]
    u = mx_kscale(H)[:, None]
    d = {}
    d["tab_words"], d["tab_scales"] = pack_weight(n((K, T)) * s, "e4m3")
    d["offs"] = striped(np.random.permutation(T)[:S])
    d["offs2"] = striped(np.random.permutation(T2)[:S])
    d["offs3"] = striped(np.random.permutation(T2)[:P])
    d["w1"] = (n((K, H)) / s * u.T / K ** 0.5).astype(np.float32)
    d["w4_words"], d["w4_scales"] = pack_weight(0.55 * n((K, H)) / s / K ** 0.5, "e2m1")
    d["wgs"] = np.exp(0.3 * n((128, S))).astype(np.float32)
    d["page0"] = (n((H, T2)) * u).astype(np.float32)
    d["lo"] = (-0.6 * np.exp(0.3 * n(H)) * u[:, 0]).astype(np.float32)
    d["hi"] = (0.7 * np.exp(0.3 * n(H)) * u[:, 0]).astype(np.float32)
    d["gain"] = (4.0 * np.exp(0.3 * n(H)) / u[:, 0] ** 2 / H ** 0.5).astype(np.float32)
    d["gm"] = n((T2, P)).astype(np.float32)
    return d


def reference(tab_words, tab_scales, offs, offs2, offs3, w1, w4_words, w4_scales,
              wgs, page0, lo, hi, gain, gm):
    v = unpack_weight(tab_words, tab_scales, "e4m3")[:, unstriped(offs)]
    a = mxq(f64(w1), 0, "e4m3").T @ v
    b = unpack_weight(w4_words, w4_scales, "e2m1").T @ v
    h = a * np.cos(b)
    page = f64(page0).copy()
    page[:, unstriped(offs2)] = np.tile(f64(wgs), (H // 128, 1)) * h
    x = page[:, unstriped(offs3)]
    x = np.minimum(np.maximum(x, f64(lo)[:, None]), f64(hi)[:, None])
    x = x * f64(gain)[:, None]
    e = mxq(page, 0, "e4m3").T @ mxq(x, 0, "e4m3")
    return 1.0 / (1.0 + np.exp(-e)) * f64(gm)

@@ -1,0 +1,265 @@
+from contextlib import ExitStack
+
+import concourse.mybir as mybir
+
+K, T, S, H, T2, NP = 1024, 2048, 512, 1024, 1024, 512
+FLOPS = 2 * K * H * S * 2 + 2 * H * T2 * NP
+
+F32 = mybir.dt.float32
+BF16 = mybir.dt.bfloat16
+I32 = mybir.dt.int32
+U32 = mybir.dt.uint32
+U16 = mybir.dt.uint16
+U8 = mybir.dt.uint8
+FP8X4 = mybir.dt.float8_e4m3fn_x4
+FP4X4 = mybir.dt.float4_e2m1fn_x4
+ALU = mybir.AluOpType
+ACT = mybir.ActivationFunctionType
+
+P = 128
+PACK = 4
+PASS = P * PACK
+PAGE_CHUNK = 256
+
+
+def tile_list_tree_ring_matching_kernel(
+    tc, tab_words, tab_scales, offs, offs2, offs3, w1, w4_words, w4_scales, wgs, page0, lo, hi, gain, gm, out
+):
+    nc = tc.nc
+    with ExitStack() as ctx:
+        lists = ctx.enter_context(tc.tile_pool(name="lists", bufs=1))
+        keep = ctx.enter_context(tc.tile_pool(name="keep", bufs=1))
+        ring = ctx.enter_context(tc.tile_pool(name="ring", bufs=2))
+        psum = ctx.enter_context(tc.psum_pool(name="psum", bufs=8))
+
+        def kept(name, shape, dtype):
+            return keep.tile(shape, dtype, name=name, align_bytes=64)
+
+        idx = lists.tile([P, S // 16], U16, name="idx")
+        idx2 = lists.tile([P, S // 16], U16, name="idx2")
+        idx3 = lists.tile([P, NP // 16], U16, name="idx3")
+
+        tab_w = [kept("tab_w%d" % a, [P, T], I32) for a in range(2)]
+        tab_s = kept("tab_s", [P, 2, T], U8)
+        w4_w = [kept("w4_w%d" % b, [P, 2, 2 * PASS], U8) for b in range(2)]
+        w4_s = kept("w4_s", [P, 2, H], U8)
+        wgs_sb = kept("wgs_sb", [P, PACK, S], F32)
+        page = [[kept("page%d%d" % (b, t), [P, T2], F32) for t in range(PACK)] for b in range(2)]
+        lo_sb = kept("lo_sb", [P, 2, PACK], F32)
+        hi_sb = kept("hi_sb", [P, 2, PACK], F32)
+        gain_sb = kept("gain_sb", [P, 2, PACK], F32)
+
+        nc.vector.memset(tab_s[:].rearrange("p a t -> p (a t)").bitcast(I32), 0)
+        nc.gpsimd.memset(w4_s[:].rearrange("p a t -> p (a t)").bitcast(I32), 0)
+
+        w1_raw = {}
+
+        def load_w1(a, b):
+            raw = ring.tile([P, PACK, PASS], F32, name="w1_raw", tag="big", bufs=4, align_bytes=64)
+            rows = w1[a * PASS : (a + 1) * PASS, b * PASS : (b + 1) * PASS]
+            nc.sync.dma_start(out=raw[:], in_=rows.rearrange("(p j) c -> p j c", j=PACK))
+            w1_raw[a, b] = raw
+
+        def load_w4(b):
+            src = w4_words.rearrange("a p c -> p a c")[:, :, 2 * PASS * b : 2 * PASS * (b + 1)]
+            nc.sync.dma_start(out=w4_w[b][:].bitcast(I32), in_=src.bitcast(I32))
+
+        def load_page(b, t):
+            rows = page0[b * PASS : (b + 1) * PASS, :].rearrange("(p t) m -> p t m", t=PACK)
+            nc.sync.dma_start(out=page[b][t][:], in_=rows[:, t, :])
+
+        def load_table(a):
+            nc.sync.dma_start(out=tab_w[a][:], in_=tab_words[a].rearrange("p t i -> p (t i)").bitcast(I32))
+
+        def load_scale_rows(dst, src):
+            rows = src.rearrange("a q c -> q a c")
+            for quad in range(4):
+                nc.sync.dma_start(
+                    out=dst[32 * quad : 32 * quad + 4, :, :].bitcast(I32),
+                    in_=rows[4 * quad : 4 * quad + 4, :, :].bitcast(I32),
+                )
+
+        nc.sync.dma_start(idx[:], offs)
+        load_table(0)
+        load_scale_rows(tab_s, tab_scales)
+        load_table(1)
+        load_scale_rows(w4_s, w4_scales)
+        load_w4(0)
+        load_w1(0, 0)
+        load_page(0, 0)
+        nc.sync.dma_start(idx2[:], offs2)
+        load_w1(1, 0)
+        for quad in (0, 2, 1, 3):
+            nc.sync.dma_start(
+                out=wgs_sb[32 * quad : 32 * quad + 32, :, :], in_=wgs.rearrange("(p t) j -> p t j", t=PACK)
+            )
+        nc.sync.dma_start(idx3[:], offs3)
+        for dst, src in ((lo_sb, lo), (hi_sb, hi), (gain_sb, gain)):
+            nc.sync.dma_start(out=dst[:], in_=src.rearrange("(b p t) -> p b t", b=2, t=PACK))
+        load_page(0, 1)
+        load_page(0, 2)
+        load_w4(1)
+        load_w1(0, 1)
+        load_w1(1, 1)
+        load_page(0, 3)
+        for t in range(PACK):
+            load_page(1, t)
+        gm_sb = []
+        for half in range(2):
+            g = ring.tile([P, PACK, NP], F32, name="gm_sb", tag="big", bufs=4, align_bytes=64)
+            rows = gm[half * PASS : (half + 1) * PASS, :]
+            nc.sync.dma_start(out=g[:], in_=rows.rearrange("(c p) j -> p c j", p=P))
+            gm_sb.append(g)
+
+        v_w = [kept("v_w%d" % a, [P, S], U32) for a in range(2)]
+        v_s = [kept("v_s%d" % a, [P, S], U8) for a in range(2)]
+        for a in range(2):
+            nc.vector.tensor_copy(v_w[a][:], tab_w[a][:].bitcast(U32).indirect(idx[:]))
+            nc.vector.tensor_copy(v_s[a][:], tab_s[:, a, :].indirect(idx[:]))
+
+        w4p_w, w4p_s, w1q_w, w1q_s = {}, {}, {}, {}
+
+        def deal_w4(b):
+            words = kept("w4p_w%d" % b, [P, 2, 2 * PASS], U8)
+            scales = kept("w4p_s%d" % b, [P, 2, PASS], U8)
+            nc.vector.tensor_copy(
+                words[:].bitcast(U16).rearrange("p a (t m) -> p a t m", t=PACK),
+                w4_w[b][:].bitcast(U16).rearrange("p a (m t) -> p a t m", t=PACK),
+            )
+            nc.vector.tensor_copy(
+                scales[:].rearrange("p a (t m) -> p a t m", t=PACK),
+                w4_s[:, :, b * PASS : (b + 1) * PASS].rearrange("p a (m t) -> p a t m", t=PACK),
+            )
+            w4p_w[b], w4p_s[b] = words, scales
+
+        def quantise_w1(a, b, on_vector):
+            grouped = ring.tile([P, PACK * PASS], BF16, name="w1_bf", align_bytes=64)
+            dst = grouped[:].rearrange("p (t m j) -> p m j t", t=PACK, j=PACK)
+            src = w1_raw[a, b][:].rearrange("p j (m t) -> p m j t", t=PACK)
+            if on_vector:
+                nc.vector.tensor_scalar(dst, src, -2.0, None, ALU.mult)
+            else:
+                nc.scalar.activation(dst, src, ACT.Copy, scale=-2.0)
+            words = kept("w1q_w%d%d" % (a, b), [P, PASS], U32)
+            scales = kept("w1q_s%d%d" % (a, b), [P, PASS], U8)
+            nc.vector.quantize_mx(out=words[:].bitcast(FP8X4), scales=scales[:], in_=grouped[:])
+            w1q_w[a, b], w1q_s[a, b] = words, scales
+
+        def features(b, t):
+            cols = slice(t * P, (t + 1) * P)
+            angle = psum.tile([P, S], F32, name="angle", tag="bank")
+            for a in range(2):
+                nc.tensor.matmul_mx(
+                    out=angle[:],
+                    lhsT=w4p_w[b][:, a, 2 * t * P : 2 * (t + 1) * P].bitcast(FP4X4),
+                    lhsT_scale=w4p_s[b][:, a, cols],
+                    rhs=v_w[a][:].bitcast(FP8X4),
+                    rhs_scale=v_s[a][:],
+                    start=(a == 0),
+                    stop=(a == 1),
+                )
+            amp = psum.tile([P, S], F32, name="amp", tag="bank")
+            for a in range(2):
+                nc.tensor.matmul_mx(
+                    out=amp[:],
+                    lhsT=w1q_w[a, b][:, cols].bitcast(FP8X4),
+                    lhsT_scale=w1q_s[a, b][:, cols],
+                    rhs=v_w[a][:].bitcast(FP8X4),
+                    rhs_scale=v_s[a][:],
+                    start=(a == 0),
+                    stop=(a == 1),
+                )
+            sin_half = ring.tile([P, S], F32, name="sin_half", tag="act", bufs=3)
+            nc.scalar.activation(sin_half[:], angle[:], ACT.Sin, scale=0.5)
+            sin_sq = ring.tile([P, S], F32, name="sin_sq", bufs=3)
+            nc.scalar.activation(sin_sq[:], sin_half[:], ACT.Square)
+            h = ring.tile([P, S], F32, name="h", tag="h", bufs=8)
+            nc.vector.scalar_tensor_tensor(h[:], sin_sq[:], 0.5, amp[:], ALU.subtract, ALU.mult)
+            return h
+
+        page_planes = [kept("page_planes%d" % b, [P, PACK, T2], BF16) for b in range(2)]
+        x_planes = [kept("x_planes%d" % b, [P, PACK, NP], BF16) for b in range(2)]
+
+        def place_and_pick(b, t, h):
+            nc.vector.tensor_tensor(page[b][t][:].indirect(idx2[:]), h[:], wgs_sb[:, t, :], ALU.mult)
+            picked = ring.tile([P, NP], F32, name="picked")
+            nc.vector.tensor_copy(picked[:], page[b][t][:].indirect(idx3[:]))
+            nc.scalar.copy(page_planes[b][:, t, :], page[b][t][:])
+            clipped = ring.tile([P, NP], F32, name="clipped")
+            nc.vector.tensor_scalar(
+                clipped[:], picked[:], lo_sb[:, b, t : t + 1], hi_sb[:, b, t : t + 1], ALU.max, ALU.min
+            )
+            nc.scalar.activation(x_planes[b][:, t, :], clipped[:], ACT.Copy, scale=gain_sb[:, b, t : t + 1])
+
+        x_w = [kept("x_w%d" % b, [P, NP], U32) for b in range(2)]
+        x_s = [kept("x_s%d" % b, [P, NP], U8) for b in range(2)]
+        chunks = T2 // PAGE_CHUNK
+        page_w = [[kept("page_w%d%d" % (b, c), [P, PAGE_CHUNK], U32) for c in range(chunks)] for b in range(2)]
+        page_s = [[kept("page_s%d%d" % (b, c), [P, PAGE_CHUNK], U8) for c in range(chunks)] for b in range(2)]
+
+        def weave(copy, dst, src):
+            copy(dst.rearrange("p (c i t) -> p c t i", i=4, t=PACK), src.rearrange("p t (c i) -> p c t i", i=4))
+
+        def quantise_x(b):
+            woven = ring.tile([P, PACK * NP], BF16, name="x_woven", align_bytes=64)
+            weave(nc.vector.tensor_copy if b == 1 else nc.scalar.copy, woven[:], x_planes[b][:])
+            nc.vector.quantize_mx(out=x_w[b][:].bitcast(FP8X4), scales=x_s[b][:], in_=woven[:])
+
+        def quantise_page(b, c):
+            woven = ring.tile([P, PACK * PAGE_CHUNK], BF16, name="page_woven", align_bytes=64, bufs=4)
+            weave(nc.scalar.copy, woven[:], page_planes[b][:, :, c * PAGE_CHUNK : (c + 1) * PAGE_CHUNK])
+            nc.vector.quantize_mx(out=page_w[b][c][:].bitcast(FP8X4), scales=page_s[b][c][:], in_=woven[:])
+
+        scores = {}
+
+        def score_pass(b, mt):
+            if b == 0:
+                scores[mt] = psum.tile([P, NP], F32, name="score", tag="bank")
+            c, first = divmod(mt * P, PAGE_CHUNK)
+            cols = slice(first, first + P)
+            nc.tensor.matmul_mx(
+                out=scores[mt][:],
+                lhsT=page_w[b][c][:, cols].bitcast(FP8X4),
+                lhsT_scale=page_s[b][c][:, cols],
+                rhs=x_w[b][:].bitcast(FP8X4),
+                rhs_scale=x_s[b][:],
+                start=(b == 0),
+                stop=(b == 1),
+            )
+
+        def finish(mt):
+            sig = ring.tile([P, NP], F32, name="sig", tag="act", bufs=3)
+            nc.scalar.activation(sig[:], scores[mt][:], ACT.Sigmoid)
+            res = ring.tile([P, NP], F32, name="res", tag="h", bufs=8)
+            nc.vector.tensor_tensor(res[:], sig[:], gm_sb[mt // PACK][:, mt % PACK, :], ALU.mult)
+            nc.sync.dma_start(out=out[mt * P : (mt + 1) * P, :], in_=res[:])
+
+        hs = {}
+        deal_w4(0)
+        quantise_w1(0, 0, False)
+        quantise_w1(1, 0, True)
+        for t in range(PACK):
+            hs[0, t] = features(0, t)
+        place_and_pick(0, 0, hs[0, 0])
+        place_and_pick(0, 1, hs[0, 1])
+        deal_w4(1)
+        quantise_w1(0, 1, False)
+        quantise_w1(1, 1, False)
+        place_and_pick(0, 2, hs[0, 2])
+        for t in range(PACK):
+            hs[1, t] = features(1, t)
+        place_and_pick(0, 3, hs[0, 3])
+        place_and_pick(1, 0, hs[1, 0])
+        quantise_x(0)
+        for c in range(chunks):
+            quantise_page(0, c)
+        for mt in range(T2 // P):
+            score_pass(0, mt)
+        for t in range(1, PACK):
+            place_and_pick(1, t, hs[1, t])
+        quantise_x(1)
+        for c in range(chunks):
+            quantise_page(1, c)
+            for mt in range(c * PAGE_CHUNK // P, (c + 1) * PAGE_CHUNK // P):
+                score_pass(1, mt)
+                finish(mt)

@@ -30,7 +30,7 @@ def tile_list_tree_ring_matching_kernel(
         lists = ctx.enter_context(tc.tile_pool(name="lists", bufs=1))
         keep = ctx.enter_context(tc.tile_pool(name="keep", bufs=1))
         ring = ctx.enter_context(tc.tile_pool(name="ring", bufs=2))
-        psum = ctx.enter_context(tc.psum_pool(name="psum", bufs=8))
+        psum = ctx.enter_context(tc.psum_pool(name="psum", bufs=1))
 
         def kept(name, shape, dtype):
             return keep.tile(shape, dtype, name=name, align_bytes=64)
@@ -42,15 +42,16 @@ def tile_list_tree_ring_matching_kernel(
         tab_w = [kept("tab_w%d" % a, [P, T], I32) for a in range(2)]
         tab_s = kept("tab_s", [P, 2, T], U8)
         w4_w = [kept("w4_w%d" % b, [P, 2, 2 * PASS], U8) for b in range(2)]
-        w4_s = kept("w4_s", [P, 2, H], U8)
-        wgs_sb = kept("wgs_sb", [P, PACK, S], F32)
+        w4_s = [kept("w4_s%d" % b, [P, 2, PASS], U8) for b in range(2)]
+        wgs_sb = [kept("wgs_sb%d" % half, [P, 2, S], F32) for half in range(2)]
         page = [[kept("page%d%d" % (b, t), [P, T2], F32) for t in range(PACK)] for b in range(2)]
         lo_sb = kept("lo_sb", [P, 2, PACK], F32)
         hi_sb = kept("hi_sb", [P, 2, PACK], F32)
         gain_sb = kept("gain_sb", [P, 2, PACK], F32)
 
         nc.vector.memset(tab_s[:].rearrange("p a t -> p (a t)").bitcast(I32), 0)
-        nc.gpsimd.memset(w4_s[:].rearrange("p a t -> p (a t)").bitcast(I32), 0)
+        for b in range(2):
+            nc.gpsimd.memset(w4_s[b][:].rearrange("p a t -> p (a t)").bitcast(I32), 0)
 
         w1_raw = {}
 
@@ -68,9 +69,6 @@ def tile_list_tree_ring_matching_kernel(
             rows = page0[b * PASS : (b + 1) * PASS, :].rearrange("(p t) m -> p t m", t=PACK)
             nc.sync.dma_start(out=page[b][t][:], in_=rows[:, t, :])
 
-        def load_table(a):
-            nc.sync.dma_start(out=tab_w[a][:], in_=tab_words[a].rearrange("p t i -> p (t i)").bitcast(I32))
-
         def load_scale_rows(dst, src):
             rows = src.rearrange("a q c -> q a c")
             for quad in range(4):
@@ -79,28 +77,38 @@ def tile_list_tree_ring_matching_kernel(
                     in_=rows[4 * quad : 4 * quad + 4, :, :].bitcast(I32),
                 )
 
+        def load_wgs(half):
+            planes = slice(2 * half, 2 * half + 2)
+            for quad in (0, 2, 1, 3):
+                nc.sync.dma_start(
+                    out=wgs_sb[half][32 * quad : 32 * quad + 32, :, :],
+                    in_=wgs.rearrange("(p t) j -> p t j", t=PACK)[:, planes, :],
+                )
+
+        def load_table(a):
+            nc.sync.dma_start(out=tab_w[a][:], in_=tab_words[a].rearrange("p t i -> p (t i)").bitcast(I32))
+
         nc.sync.dma_start(idx[:], offs)
         load_table(0)
         load_scale_rows(tab_s, tab_scales)
         load_table(1)
-        load_scale_rows(w4_s, w4_scales)
         load_w4(0)
+        load_scale_rows(w4_s[0], w4_scales[:, :, :PASS])
         load_w1(0, 0)
+        load_w1(1, 0)
         load_page(0, 0)
         nc.sync.dma_start(idx2[:], offs2)
-        load_w1(1, 0)
-        for quad in (0, 2, 1, 3):
-            nc.sync.dma_start(
-                out=wgs_sb[32 * quad : 32 * quad + 32, :, :], in_=wgs.rearrange("(p t) j -> p t j", t=PACK)
-            )
+        load_wgs(0)
         nc.sync.dma_start(idx3[:], offs3)
+        load_page(0, 1)
         for dst, src in ((lo_sb, lo), (hi_sb, hi), (gain_sb, gain)):
             nc.sync.dma_start(out=dst[:], in_=src.rearrange("(b p t) -> p b t", b=2, t=PACK))
-        load_page(0, 1)
-        load_page(0, 2)
-        load_w4(1)
         load_w1(0, 1)
         load_w1(1, 1)
+        load_w4(1)
+        load_scale_rows(w4_s[1], w4_scales[:, :, PASS:])
+        load_wgs(1)
+        load_page(0, 2)
         load_page(0, 3)
         for t in range(PACK):
             load_page(1, t)
@@ -117,7 +125,7 @@ def tile_list_tree_ring_matching_kernel(
             nc.vector.tensor_copy(v_w[a][:], tab_w[a][:].bitcast(U32).indirect(idx[:]))
             nc.vector.tensor_copy(v_s[a][:], tab_s[:, a, :].indirect(idx[:]))
 
-        w4p_w, w4p_s, w1q_w, w1q_s = {}, {}, {}, {}
+        w4p_w, w4p_s, w1q_w, w1q_s, w1_rounded = {}, {}, {}, {}, {}
 
         def deal_w4(b):
             words = kept("w4p_w%d" % b, [P, 2, 2 * PASS], U8)
@@ -128,37 +136,56 @@ def tile_list_tree_ring_matching_kernel(
             )
             nc.vector.tensor_copy(
                 scales[:].rearrange("p a (t m) -> p a t m", t=PACK),
-                w4_s[:, :, b * PASS : (b + 1) * PASS].rearrange("p a (m t) -> p a t m", t=PACK),
+                w4_s[b][:].rearrange("p a (m t) -> p a t m", t=PACK),
             )
             w4p_w[b], w4p_s[b] = words, scales
 
-        def quantise_w1(a, b, on_vector):
-            grouped = ring.tile([P, PACK * PASS], BF16, name="w1_bf", align_bytes=64)
+        def quantise_w1(a, b, vector_columns, pieces=((0, PASS),)):
+            grouped = ring.tile([P, PACK * PASS], BF16, name="w1_bf", tag="w1_bf%d%d" % (a, b), bufs=1, align_bytes=64)
             dst = grouped[:].rearrange("p (t m j) -> p m j t", t=PACK, j=PACK)
             src = w1_raw[a, b][:].rearrange("p j (m t) -> p m j t", t=PACK)
-            if on_vector:
-                nc.vector.tensor_scalar(dst, src, -2.0, None, ALU.mult)
-            else:
-                nc.scalar.activation(dst, src, ACT.Copy, scale=-2.0)
+            if vector_columns > 0:
+                nc.vector.tensor_scalar(dst[:, :vector_columns], src[:, :vector_columns], -2.0, None, ALU.mult)
+            if vector_columns < P:
+                nc.scalar.activation(dst[:, vector_columns:], src[:, vector_columns:], ACT.Copy, scale=-2.0)
             words = kept("w1q_w%d%d" % (a, b), [P, PASS], U32)
             scales = kept("w1q_s%d%d" % (a, b), [P, PASS], U8)
-            nc.vector.quantize_mx(out=words[:].bitcast(FP8X4), scales=scales[:], in_=grouped[:])
+            for first, last in pieces:
+                nc.vector.quantize_mx(
+                    out=words[:, first:last].bitcast(FP8X4),
+                    scales=scales[:, first:last],
+                    in_=grouped[:, PACK * first : PACK * last],
+                )
             w1q_w[a, b], w1q_s[a, b] = words, scales
+            w1_rounded[a, b] = grouped
 
-        def features(b, t):
-            cols = slice(t * P, (t + 1) * P)
-            angle = psum.tile([P, S], F32, name="angle", tag="bank")
+        sin_sq = {}
+
+        def angle_part(b, t, reuse=None):
+            angle = psum.tile([P, S], F32, name="angle", tag="angle", bufs=3)
             for a in range(2):
                 nc.tensor.matmul_mx(
                     out=angle[:],
                     lhsT=w4p_w[b][:, a, 2 * t * P : 2 * (t + 1) * P].bitcast(FP4X4),
-                    lhsT_scale=w4p_s[b][:, a, cols],
+                    lhsT_scale=w4p_s[b][:, a, t * P : (t + 1) * P],
                     rhs=v_w[a][:].bitcast(FP8X4),
                     rhs_scale=v_s[a][:],
                     start=(a == 0),
                     stop=(a == 1),
                 )
-            amp = psum.tile([P, S], F32, name="amp", tag="bank")
+            if reuse is None:
+                sin_half = ring.tile([P, S], F32, name="sin_half", tag="act", bufs=4)[:]
+            else:
+                sin_half = reuse
+            nc.scalar.activation(sin_half, angle[:], ACT.Sin, scale=0.5)
+            sin_sq[b, t] = ring.tile([P, S], F32, name="sin_sq", tag="sin_sq", bufs=8)
+            nc.scalar.activation(sin_sq[b, t][:], sin_half, ACT.Square)
+
+        features = {}
+
+        def feature(b, t, reuse=None):
+            cols = slice(t * P, (t + 1) * P)
+            amp = psum.tile([P, S], F32, name="amp", tag="amp", bufs=5)
             for a in range(2):
                 nc.tensor.matmul_mx(
                     out=amp[:],
@@ -169,31 +196,68 @@ def tile_list_tree_ring_matching_kernel(
                     start=(a == 0),
                     stop=(a == 1),
                 )
-            sin_half = ring.tile([P, S], F32, name="sin_half", tag="act", bufs=3)
-            nc.scalar.activation(sin_half[:], angle[:], ACT.Sin, scale=0.5)
-            sin_sq = ring.tile([P, S], F32, name="sin_sq", bufs=3)
-            nc.scalar.activation(sin_sq[:], sin_half[:], ACT.Square)
-            h = ring.tile([P, S], F32, name="h", tag="h", bufs=8)
-            nc.vector.scalar_tensor_tensor(h[:], sin_sq[:], 0.5, amp[:], ALU.subtract, ALU.mult)
-            return h
+            if reuse is None:
+                h = ring.tile([P, S], F32, name="h", tag="h", bufs=3, align_bytes=64)[:]
+            else:
+                h = reuse[:].bitcast(F32)[:, :S]
+            nc.vector.scalar_tensor_tensor(h, sin_sq[b, t][:], 0.5, amp[:], ALU.subtract, ALU.mult)
+            features[b, t] = h
 
-        page_planes = [kept("page_planes%d" % b, [P, PACK, T2], BF16) for b in range(2)]
-        x_planes = [kept("x_planes%d" % b, [P, PACK, NP], BF16) for b in range(2)]
+        page_planes = w1_raw[0, 1][:].rearrange("p j c -> p (j c)").bitcast(BF16).rearrange("p (t m) -> p t m", t=PACK)
+        x_planes = w1_raw[1, 1][:, :2, :].rearrange("p j c -> p (j c)").bitcast(BF16).rearrange("p (t m) -> p t m", t=PACK)
+        chunks = T2 // PAGE_CHUNK
+        first_woven = [kept("first_woven%d" % c, [P, PACK * PAGE_CHUNK], BF16) for c in range(chunks)]
+        last_woven = [kept("last_woven%d" % c, [P, PAGE_CHUNK, PACK], BF16) for c in range(chunks)]
+        last_x = [kept("last_x%d" % u, [P, NP // 2, PACK], BF16) for u in range(2)]
+        picked, clipped = {}, {}
 
-        def place_and_pick(b, t, h):
-            nc.vector.tensor_tensor(page[b][t][:].indirect(idx2[:]), h[:], wgs_sb[:, t, :], ALU.mult)
-            picked = ring.tile([P, NP], F32, name="picked")
-            nc.vector.tensor_copy(picked[:], page[b][t][:].indirect(idx3[:]))
-            nc.scalar.copy(page_planes[b][:, t, :], page[b][t][:])
-            clipped = ring.tile([P, NP], F32, name="clipped")
-            nc.vector.tensor_scalar(
-                clipped[:], picked[:], lo_sb[:, b, t : t + 1], hi_sb[:, b, t : t + 1], ALU.max, ALU.min
+        def place(b, t):
+            nc.vector.tensor_tensor(
+                page[b][t][:].indirect(idx2[:]), features[b, t], wgs_sb[t // 2][:, t % 2, :], ALU.mult
             )
-            nc.scalar.activation(x_planes[b][:, t, :], clipped[:], ACT.Copy, scale=gain_sb[:, b, t : t + 1])
+
+        def pick(b, t, parts=1):
+            picked[b, t] = ring.tile([P, NP], F32, name="picked", bufs=3)
+            width = NP // parts
+            for u in range(parts):
+                entries = idx3[:, u * width // 16 : (u + 1) * width // 16]
+                nc.vector.tensor_copy(picked[b, t][:, u * width : (u + 1) * width], page[b][t][:].indirect(entries))
+
+        def clip(b, t, parts=1):
+            clipped[b, t] = ring.tile([P, NP], F32, name="clipped", bufs=5)
+            width = NP // parts
+            for u in range(parts):
+                cols = slice(u * width, (u + 1) * width)
+                nc.vector.tensor_scalar(
+                    clipped[b, t][:, cols],
+                    picked[b, t][:, cols],
+                    lo_sb[:, b, t : t + 1],
+                    hi_sb[:, b, t : t + 1],
+                    ALU.max,
+                    ALU.min,
+                )
+
+        def round_page(b, t):
+            if b == 0:
+                nc.scalar.copy(page_planes[:, t, :], page[b][t][:])
+            else:
+                for c in range(chunks):
+                    nc.scalar.copy(last_woven[c][:, :, t], page[b][t][:, c * PAGE_CHUNK : (c + 1) * PAGE_CHUNK])
+
+        def round_x(b, t):
+            factor = gain_sb[:, b, t : t + 1]
+            if b == 0:
+                nc.scalar.activation(x_planes[:, t, :], clipped[b, t][:], ACT.Copy, scale=factor)
+            else:
+                for u in range(2):
+                    src = clipped[b, t][:, u * NP // 2 : (u + 1) * NP // 2]
+                    if t < 2:
+                        nc.scalar.activation(last_x[u][:, :, t], src, ACT.Copy, scale=factor)
+                    else:
+                        nc.vector.tensor_scalar(last_x[u][:, :, t], src, factor, None, ALU.mult)
 
         x_w = [kept("x_w%d" % b, [P, NP], U32) for b in range(2)]
         x_s = [kept("x_s%d" % b, [P, NP], U8) for b in range(2)]
-        chunks = T2 // PAGE_CHUNK
         page_w = [[kept("page_w%d%d" % (b, c), [P, PAGE_CHUNK], U32) for c in range(chunks)] for b in range(2)]
         page_s = [[kept("page_s%d%d" % (b, c), [P, PAGE_CHUNK], U8) for c in range(chunks)] for b in range(2)]
 
@@ -201,20 +265,34 @@ def tile_list_tree_ring_matching_kernel(
             copy(dst.rearrange("p (c i t) -> p c t i", i=4, t=PACK), src.rearrange("p t (c i) -> p c t i", i=4))
 
         def quantise_x(b):
-            woven = ring.tile([P, PACK * NP], BF16, name="x_woven", align_bytes=64)
-            weave(nc.vector.tensor_copy if b == 1 else nc.scalar.copy, woven[:], x_planes[b][:])
-            nc.vector.quantize_mx(out=x_w[b][:].bitcast(FP8X4), scales=x_s[b][:], in_=woven[:])
+            if b == 0:
+                woven = ring.tile([P, PACK * NP], BF16, name="x_woven", align_bytes=64, bufs=1)
+                weave(nc.scalar.copy, woven[:], x_planes)
+                nc.vector.quantize_mx(out=x_w[b][:].bitcast(FP8X4), scales=x_s[b][:], in_=woven[:])
+            else:
+                for u in range(2):
+                    cols = slice(u * NP // 2, (u + 1) * NP // 2)
+                    nc.vector.quantize_mx(
+                        out=x_w[b][:, cols].bitcast(FP8X4),
+                        scales=x_s[b][:, cols],
+                        in_=last_x[u][:].rearrange("p j t -> p (j t)"),
+                    )
 
         def quantise_page(b, c):
-            woven = ring.tile([P, PACK * PAGE_CHUNK], BF16, name="page_woven", align_bytes=64, bufs=4)
-            weave(nc.scalar.copy, woven[:], page_planes[b][:, :, c * PAGE_CHUNK : (c + 1) * PAGE_CHUNK])
-            nc.vector.quantize_mx(out=page_w[b][c][:].bitcast(FP8X4), scales=page_s[b][c][:], in_=woven[:])
+            if b == 0:
+                woven = first_woven[c]
+                weave(nc.scalar.copy, woven[:], page_planes[:, :, c * PAGE_CHUNK : (c + 1) * PAGE_CHUNK])
+                rounded = woven[:]
+            else:
+                rounded = last_woven[c][:].rearrange("p m t -> p (m t)")
+            nc.vector.quantize_mx(out=page_w[b][c][:].bitcast(FP8X4), scales=page_s[b][c][:], in_=rounded)
 
         scores = {}
 
         def score_pass(b, mt):
             if b == 0:
-                scores[mt] = psum.tile([P, NP], F32, name="score", tag="bank")
+                tag, bufs = ("angle", 3) if mt < 3 else ("amp", 5)
+                scores[mt] = psum.tile([P, NP], F32, name="score", tag=tag, bufs=bufs)
             c, first = divmod(mt * P, PAGE_CHUNK)
             cols = slice(first, first + P)
             nc.tensor.matmul_mx(
@@ -228,38 +306,76 @@ def tile_list_tree_ring_matching_kernel(
             )
 
         def finish(mt):
-            sig = ring.tile([P, NP], F32, name="sig", tag="act", bufs=3)
+            sig = ring.tile([P, NP], F32, name="sig", tag="act", bufs=4)
             nc.scalar.activation(sig[:], scores[mt][:], ACT.Sigmoid)
-            res = ring.tile([P, NP], F32, name="res", tag="h", bufs=8)
+            res = ring.tile([P, NP], F32, name="res", tag="sin_sq", bufs=8)
             nc.vector.tensor_tensor(res[:], sig[:], gm_sb[mt // PACK][:, mt % PACK, :], ALU.mult)
             nc.sync.dma_start(out=out[mt * P : (mt + 1) * P, :], in_=res[:])
 
-        hs = {}
         deal_w4(0)
-        quantise_w1(0, 0, False)
-        quantise_w1(1, 0, True)
-        for t in range(PACK):
-            hs[0, t] = features(0, t)
-        place_and_pick(0, 0, hs[0, 0])
-        place_and_pick(0, 1, hs[0, 1])
+        quantise_w1(0, 0, 0)
+        angle_part(0, 0, w1_raw[0, 0][:, 0, :])
+        quantise_w1(1, 0, P, ((0, P), (P, PASS)))
+        feature(0, 0)
+        for t in range(1, PACK):
+            angle_part(0, t, w1_raw[0, 0][:, t, :])
+        feature(0, 1)
+        place(0, 0)
+        pick(0, 0)
+        feature(0, 2)
+        place(0, 1)
+        clip(0, 0)
+        pick(0, 1)
+        quantise_w1(0, 1, 0)
+        quantise_w1(1, 1, 0)
         deal_w4(1)
-        quantise_w1(0, 1, False)
-        quantise_w1(1, 1, False)
-        place_and_pick(0, 2, hs[0, 2])
         for t in range(PACK):
-            hs[1, t] = features(1, t)
-        place_and_pick(0, 3, hs[0, 3])
-        place_and_pick(1, 0, hs[1, 0])
-        quantise_x(0)
-        for c in range(chunks):
+            angle_part(1, t)
+        place(0, 2)
+        clip(0, 1)
+        pick(0, 2)
+        feature(0, 3, w1_rounded[1, 1])
+        clip(0, 2)
+        place(0, 3)
+        feature(1, 0)
+        pick(0, 3)
+        feature(1, 1)
+        feature(1, 2)
+        clip(0, 3)
+        place(1, 0)
+        for t in range(PACK - 1):
+            round_page(0, t)
+            round_x(0, t)
+        round_page(0, 3)
+        pick(1, 0)
+        place(1, 1)
+        clip(1, 0)
+        pick(1, 1)
+        for c in range(chunks - 1):
             quantise_page(0, c)
+        round_x(0, 3)
+        quantise_x(0)
+        quantise_page(0, chunks - 1)
+        place(1, 2)
+        clip(1, 1)
+        pick(1, 2)
+        feature(1, 3, first_woven[chunks - 1])
+        clip(1, 2)
         for mt in range(T2 // P):
             score_pass(0, mt)
-        for t in range(1, PACK):
-            place_and_pick(1, t, hs[1, t])
+        for t in range(3):
+            round_page(1, t)
+            round_x(1, t)
+        place(1, 3)
+        round_page(1, 3)
+        pick(1, 3, 2)
+        clip(1, 3, 2)
+        round_x(1, 3)
+        quantise_page(1, 0)
         quantise_x(1)
         for c in range(chunks):
-            quantise_page(1, c)
+            if c > 0:
+                quantise_page(1, c)
             for mt in range(c * PAGE_CHUNK // P, (c + 1) * PAGE_CHUNK // P):
                 score_pass(1, mt)
                 finish(mt)

@@ -43,7 +43,7 @@ def tile_list_tree_ring_matching_kernel(
         tab_s = kept("tab_s", [P, 2, T], U8)
         w4_w = [kept("w4_w%d" % b, [P, 2, 2 * PASS], U8) for b in range(2)]
         w4_s = [kept("w4_s%d" % b, [P, 2, PASS], U8) for b in range(2)]
-        wgs_sb = [kept("wgs_sb%d" % half, [P, 2, S], F32) for half in range(2)]
+        wgs_sb = kept("wgs_sb", [P, PACK, S], F32)
         page = [[kept("page%d%d" % (b, t), [P, T2], F32) for t in range(PACK)] for b in range(2)]
         lo_sb = kept("lo_sb", [P, 2, PACK], F32)
         hi_sb = kept("hi_sb", [P, 2, PACK], F32)
@@ -55,10 +55,15 @@ def tile_list_tree_ring_matching_kernel(
 
         w1_raw = {}
 
+        stage = kept("stage", [P, 9 * PASS], F32)
+
         def load_w1(a, b):
-            raw = ring.tile([P, PACK, PASS], F32, name="w1_raw", tag="big", bufs=4, align_bytes=64)
-            rows = w1[a * PASS : (a + 1) * PASS, b * PASS : (b + 1) * PASS]
-            nc.sync.dma_start(out=raw[:], in_=rows.rearrange("(p j) c -> p j c", j=PACK))
+            if b == 0:
+                raw = ring.tile([P, PACK, PASS], F32, name="w1_raw", tag="big", bufs=2, align_bytes=64)[:]
+            else:
+                raw = stage[:, a * PACK * PASS : (a + 1) * PACK * PASS].rearrange("p (j c) -> p j c", j=PACK)
+            rows = w1[a * PASS : (a + 1) * PASS, b * PASS : (b + 1) * PASS].rearrange("(p j) c -> p j c", j=PACK)
+            nc.sync.dma_start(out=raw, in_=rows)
             w1_raw[a, b] = raw
 
         def load_w4(b):
@@ -77,12 +82,11 @@ def tile_list_tree_ring_matching_kernel(
                     in_=rows[4 * quad : 4 * quad + 4, :, :].bitcast(I32),
                 )
 
-        def load_wgs(half):
-            planes = slice(2 * half, 2 * half + 2)
+        def load_wgs(first, last):
             for quad in (0, 2, 1, 3):
                 nc.sync.dma_start(
-                    out=wgs_sb[half][32 * quad : 32 * quad + 32, :, :],
-                    in_=wgs.rearrange("(p t) j -> p t j", t=PACK)[:, planes, :],
+                    out=wgs_sb[32 * quad : 32 * quad + 32, first:last, :],
+                    in_=wgs.rearrange("(p t) j -> p t j", t=PACK)[:, first:last, :],
                 )
 
         def load_table(a):
@@ -98,26 +102,30 @@ def tile_list_tree_ring_matching_kernel(
         load_w1(1, 0)
         load_page(0, 0)
         nc.sync.dma_start(idx2[:], offs2)
-        load_wgs(0)
-        nc.sync.dma_start(idx3[:], offs3)
+        load_wgs(0, 1)
         load_page(0, 1)
+        nc.sync.dma_start(idx3[:], offs3)
+        load_wgs(1, 2)
+        load_w1(0, 1)
         for dst, src in ((lo_sb, lo), (hi_sb, hi), (gain_sb, gain)):
             nc.sync.dma_start(out=dst[:], in_=src.rearrange("(b p t) -> p b t", b=2, t=PACK))
-        load_w1(0, 1)
         load_w1(1, 1)
         load_w4(1)
-        load_scale_rows(w4_s[1], w4_scales[:, :, PASS:])
-        load_wgs(1)
         load_page(0, 2)
+        load_scale_rows(w4_s[1], w4_scales[:, :, PASS:])
         load_page(0, 3)
-        for t in range(PACK):
-            load_page(1, t)
+        load_wgs(2, 3)
+        load_page(1, 0)
+        load_page(1, 1)
+        load_page(1, 2)
+        load_wgs(3, 4)
         gm_sb = []
         for half in range(2):
-            g = ring.tile([P, PACK, NP], F32, name="gm_sb", tag="big", bufs=4, align_bytes=64)
+            g = ring.tile([P, PACK, NP], F32, name="gm_sb", tag="big", bufs=2, align_bytes=64)
             rows = gm[half * PASS : (half + 1) * PASS, :]
             nc.sync.dma_start(out=g[:], in_=rows.rearrange("(c p) j -> p c j", p=P))
             gm_sb.append(g)
+        load_page(1, 3)
 
         v_w = [kept("v_w%d" % a, [P, S], U32) for a in range(2)]
         v_s = [kept("v_s%d" % a, [P, S], U8) for a in range(2)]
@@ -127,10 +135,10 @@ def tile_list_tree_ring_matching_kernel(
 
         w4p_w, w4p_s, w1q_w, w1q_s, w1_rounded = {}, {}, {}, {}, {}
 
-        def deal_w4(b):
+        def deal_w4(b, copy_words):
             words = kept("w4p_w%d" % b, [P, 2, 2 * PASS], U8)
             scales = kept("w4p_s%d" % b, [P, 2, PASS], U8)
-            nc.vector.tensor_copy(
+            copy_words(
                 words[:].bitcast(U16).rearrange("p a (t m) -> p a t m", t=PACK),
                 w4_w[b][:].bitcast(U16).rearrange("p a (m t) -> p a t m", t=PACK),
             )
@@ -140,14 +148,14 @@ def tile_list_tree_ring_matching_kernel(
             )
             w4p_w[b], w4p_s[b] = words, scales
 
-        def quantise_w1(a, b, vector_columns, pieces=((0, PASS),)):
+        def quantise_w1(a, b, on_vector, pieces=((0, PASS),)):
             grouped = ring.tile([P, PACK * PASS], BF16, name="w1_bf", tag="w1_bf%d%d" % (a, b), bufs=1, align_bytes=64)
             dst = grouped[:].rearrange("p (t m j) -> p m j t", t=PACK, j=PACK)
-            src = w1_raw[a, b][:].rearrange("p j (m t) -> p m j t", t=PACK)
-            if vector_columns > 0:
-                nc.vector.tensor_scalar(dst[:, :vector_columns], src[:, :vector_columns], -2.0, None, ALU.mult)
-            if vector_columns < P:
-                nc.scalar.activation(dst[:, vector_columns:], src[:, vector_columns:], ACT.Copy, scale=-2.0)
+            src = w1_raw[a, b].rearrange("p j (m t) -> p m j t", t=PACK)
+            if on_vector:
+                nc.vector.tensor_scalar(dst, src, -2.0, None, ALU.mult)
+            else:
+                nc.scalar.activation(dst, src, ACT.Copy, scale=-2.0)
             words = kept("w1q_w%d%d" % (a, b), [P, PASS], U32)
             scales = kept("w1q_s%d%d" % (a, b), [P, PASS], U8)
             for first, last in pieces:
@@ -162,7 +170,7 @@ def tile_list_tree_ring_matching_kernel(
         sin_sq = {}
 
         def angle_part(b, t, reuse=None):
-            angle = psum.tile([P, S], F32, name="angle", tag="angle", bufs=3)
+            angle = psum.tile([P, S], F32, name="angle", tag="angle", bufs=4)
             for a in range(2):
                 nc.tensor.matmul_mx(
                     out=angle[:],
@@ -185,76 +193,90 @@ def tile_list_tree_ring_matching_kernel(
 
         def feature(b, t, reuse=None):
             cols = slice(t * P, (t + 1) * P)
-            amp = psum.tile([P, S], F32, name="amp", tag="amp", bufs=5)
-            for a in range(2):
+            amp = psum.tile([P, S], F32, name="amp", tag="amp", bufs=4)
+            passes = (0, 1) if t == 0 else (1, 0)
+            for a in passes:
                 nc.tensor.matmul_mx(
                     out=amp[:],
                     lhsT=w1q_w[a, b][:, cols].bitcast(FP8X4),
                     lhsT_scale=w1q_s[a, b][:, cols],
                     rhs=v_w[a][:].bitcast(FP8X4),
                     rhs_scale=v_s[a][:],
-                    start=(a == 0),
-                    stop=(a == 1),
+                    start=(a == passes[0]),
+                    stop=(a == passes[1]),
                 )
             if reuse is None:
-                h = ring.tile([P, S], F32, name="h", tag="h", bufs=3, align_bytes=64)[:]
+                h = ring.tile([P, S], F32, name="h", tag="h", bufs=1, align_bytes=64)[:]
             else:
-                h = reuse[:].bitcast(F32)[:, :S]
+                h = reuse
             nc.vector.scalar_tensor_tensor(h, sin_sq[b, t][:], 0.5, amp[:], ALU.subtract, ALU.mult)
             features[b, t] = h
 
-        page_planes = w1_raw[0, 1][:].rearrange("p j c -> p (j c)").bitcast(BF16).rearrange("p (t m) -> p t m", t=PACK)
-        x_planes = w1_raw[1, 1][:, :2, :].rearrange("p j c -> p (j c)").bitcast(BF16).rearrange("p (t m) -> p t m", t=PACK)
+        page_planes = stage[:, 3 * PASS : 7 * PASS].bitcast(BF16).rearrange("p (t m) -> p t m", t=PACK)
+        x_planes = stage[:, 7 * PASS :].bitcast(BF16).rearrange("p (t m) -> p t m", t=PACK)
         chunks = T2 // PAGE_CHUNK
         first_woven = [kept("first_woven%d" % c, [P, PACK * PAGE_CHUNK], BF16) for c in range(chunks)]
         last_woven = [kept("last_woven%d" % c, [P, PAGE_CHUNK, PACK], BF16) for c in range(chunks)]
+        first_x = kept("first_x", [P, PACK * NP], BF16)
         last_x = [kept("last_x%d" % u, [P, NP // 2, PACK], BF16) for u in range(2)]
+        last_planes = kept("last_planes", [P, 2, T2], BF16)
+        last_x_planes = kept("last_x_planes", [P, 2, NP], BF16)
         picked, clipped = {}, {}
 
         def place(b, t):
             nc.vector.tensor_tensor(
-                page[b][t][:].indirect(idx2[:]), features[b, t], wgs_sb[t // 2][:, t % 2, :], ALU.mult
+                page[b][t][:].indirect(idx2[:]), features[b, t], wgs_sb[:, t, :], ALU.mult
             )
 
         def pick(b, t, parts=1):
-            picked[b, t] = ring.tile([P, NP], F32, name="picked", bufs=3)
+            picked[b, t] = ring.tile([P, NP], F32, name="picked", bufs=4)
             width = NP // parts
             for u in range(parts):
                 entries = idx3[:, u * width // 16 : (u + 1) * width // 16]
                 nc.vector.tensor_copy(picked[b, t][:, u * width : (u + 1) * width], page[b][t][:].indirect(entries))
 
-        def clip(b, t, parts=1):
-            clipped[b, t] = ring.tile([P, NP], F32, name="clipped", bufs=5)
+        def clip(b, t, engine, parts=1, reuse=None):
+            if reuse is None:
+                clipped[b, t] = ring.tile([P, NP], F32, name="clipped", bufs=4)[:]
+            else:
+                clipped[b, t] = reuse
             width = NP // parts
             for u in range(parts):
                 cols = slice(u * width, (u + 1) * width)
-                nc.vector.tensor_scalar(
+                engine.tensor_scalar(
                     clipped[b, t][:, cols],
                     picked[b, t][:, cols],
-                    lo_sb[:, b, t : t + 1],
                     hi_sb[:, b, t : t + 1],
-                    ALU.max,
+                    lo_sb[:, b, t : t + 1],
                     ALU.min,
+                    ALU.max,
                 )
 
         def round_page(b, t):
-            if b == 0:
-                nc.scalar.copy(page_planes[:, t, :], page[b][t][:])
-            else:
-                for c in range(chunks):
-                    nc.scalar.copy(last_woven[c][:, :, t], page[b][t][:, c * PAGE_CHUNK : (c + 1) * PAGE_CHUNK])
+            if t < (PACK - 1 if b == 0 else 2):
+                nc.scalar.copy((page_planes if b == 0 else last_planes)[:, t, :], page[b][t][:])
+                return
+            for c in range(chunks):
+                cols = slice(c * PAGE_CHUNK, (c + 1) * PAGE_CHUNK)
+                nc.scalar.copy(page_planes[:, t, cols] if b == 0 else last_woven[c][:, :, t], page[b][t][:, cols])
 
         def round_x(b, t):
             factor = gain_sb[:, b, t : t + 1]
-            if b == 0:
-                nc.scalar.activation(x_planes[:, t, :], clipped[b, t][:], ACT.Copy, scale=factor)
-            else:
-                for u in range(2):
-                    src = clipped[b, t][:, u * NP // 2 : (u + 1) * NP // 2]
-                    if t < 2:
-                        nc.scalar.activation(last_x[u][:, :, t], src, ACT.Copy, scale=factor)
-                    else:
-                        nc.vector.tensor_scalar(last_x[u][:, :, t], src, factor, None, ALU.mult)
+            if b == 0 or t < 2:
+                planes = x_planes if b == 0 else last_x_planes
+                nc.scalar.activation(planes[:, t, :], clipped[b, t], ACT.Copy, scale=factor)
+                return
+            for u in range(2):
+                src = clipped[b, t][:, u * NP // 2 : (u + 1) * NP // 2]
+                if t == 2:
+                    nc.scalar.activation(last_x[u][:, :, t], src, ACT.Copy, scale=factor)
+                else:
+                    nc.vector.tensor_scalar(last_x[u][:, :, t], src, factor, None, ALU.mult)
+
+        def weave_pair(dst, src):
+            nc.scalar.copy(
+                dst[:, :, :2].rearrange("p (c i) t -> p c t i", i=4), src.rearrange("p t (c i) -> p c t i", i=4)
+            )
 
         x_w = [kept("x_w%d" % b, [P, NP], U32) for b in range(2)]
         x_s = [kept("x_s%d" % b, [P, NP], U8) for b in range(2)]
@@ -266,7 +288,7 @@ def tile_list_tree_ring_matching_kernel(
 
         def quantise_x(b):
             if b == 0:
-                woven = ring.tile([P, PACK * NP], BF16, name="x_woven", align_bytes=64, bufs=1)
+                woven = first_x
                 weave(nc.scalar.copy, woven[:], x_planes)
                 nc.vector.quantize_mx(out=x_w[b][:].bitcast(FP8X4), scales=x_s[b][:], in_=woven[:])
             else:
@@ -291,8 +313,7 @@ def tile_list_tree_ring_matching_kernel(
 
         def score_pass(b, mt):
             if b == 0:
-                tag, bufs = ("angle", 3) if mt < 3 else ("amp", 5)
-                scores[mt] = psum.tile([P, NP], F32, name="score", tag=tag, bufs=bufs)
+                scores[mt] = psum.tile([P, NP], F32, name="score", tag="angle" if mt < 4 else "amp", bufs=4)
             c, first = divmod(mt * P, PAGE_CHUNK)
             cols = slice(first, first + P)
             nc.tensor.matmul_mx(
@@ -312,64 +333,73 @@ def tile_list_tree_ring_matching_kernel(
             nc.vector.tensor_tensor(res[:], sig[:], gm_sb[mt // PACK][:, mt % PACK, :], ALU.mult)
             nc.sync.dma_start(out=out[mt * P : (mt + 1) * P, :], in_=res[:])
 
-        deal_w4(0)
-        quantise_w1(0, 0, 0)
-        angle_part(0, 0, w1_raw[0, 0][:, 0, :])
-        quantise_w1(1, 0, P, ((0, P), (P, PASS)))
+        deal_w4(0, nc.vector.tensor_copy)
+        quantise_w1(0, 0, True)
+        angle_part(0, 0)
+        quantise_w1(1, 0, True, ((0, P), (P, PASS)))
         feature(0, 0)
         for t in range(1, PACK):
-            angle_part(0, t, w1_raw[0, 0][:, t, :])
-        feature(0, 1)
+            angle_part(0, t)
         place(0, 0)
         pick(0, 0)
-        feature(0, 2)
+        feature(0, 1, features[0, 0])
         place(0, 1)
-        clip(0, 0)
+        clip(0, 0, nc.vector)
+        feature(0, 2, features[0, 0])
         pick(0, 1)
-        quantise_w1(0, 1, 0)
-        quantise_w1(1, 1, 0)
-        deal_w4(1)
-        for t in range(PACK):
-            angle_part(1, t)
+        clip(0, 1, nc.vector)
+        quantise_w1(0, 1, False)
+        quantise_w1(1, 1, False)
+        deal_w4(1, nc.scalar.copy)
+        angle_part(1, 0)
+        angle_part(1, 1)
+        angle_part(1, 2, stage[:, 6 * PASS : 7 * PASS])
+        angle_part(1, 3, stage[:, 8 * PASS :])
         place(0, 2)
-        clip(0, 1)
+        feature(0, 3, w1_rounded[1, 1][:].bitcast(F32)[:, :S])
         pick(0, 2)
-        feature(0, 3, w1_rounded[1, 1])
-        clip(0, 2)
         place(0, 3)
-        feature(1, 0)
+        clip(0, 2, nc.vector)
         pick(0, 3)
-        feature(1, 1)
-        feature(1, 2)
-        clip(0, 3)
+        feature(1, 0, features[0, 3])
+        clip(0, 3, nc.vector)
         place(1, 0)
+        feature(1, 1, picked[0, 3][:])
         for t in range(PACK - 1):
             round_page(0, t)
             round_x(0, t)
         round_page(0, 3)
         pick(1, 0)
         place(1, 1)
-        clip(1, 0)
+        clip(1, 0, nc.vector)
+        feature(1, 2, features[1, 0])
         pick(1, 1)
-        for c in range(chunks - 1):
+        clip(1, 1, nc.vector)
+        for c in range(chunks):
             quantise_page(0, c)
         round_x(0, 3)
         quantise_x(0)
-        quantise_page(0, chunks - 1)
         place(1, 2)
-        clip(1, 1)
+        feature(1, 3, features[1, 1])
         pick(1, 2)
-        feature(1, 3, first_woven[chunks - 1])
-        clip(1, 2)
+        clip(1, 2, nc.vector)
         for mt in range(T2 // P):
             score_pass(0, mt)
-        for t in range(3):
-            round_page(1, t)
-            round_x(1, t)
+        round_page(1, 0)
+        round_page(1, 1)
+        round_x(1, 0)
+        for c in range(chunks):
+            if c == chunks - 1:
+                round_x(1, 1)
+            weave_pair(last_woven[c], last_planes[:, :, c * PAGE_CHUNK : (c + 1) * PAGE_CHUNK])
+        for u in range(2):
+            weave_pair(last_x[u], last_x_planes[:, :, u * NP // 2 : (u + 1) * NP // 2])
+        round_page(1, 2)
+        round_x(1, 2)
         place(1, 3)
         round_page(1, 3)
         pick(1, 3, 2)
-        clip(1, 3, 2)
+        clip(1, 3, nc.vector, 2, clipped[1, 2])
         round_x(1, 3)
         quantise_page(1, 0)
         quantise_x(1)

@@ -148,29 +148,25 @@ def tile_list_tree_ring_matching_kernel(
             )
             w4p_w[b], w4p_s[b] = words, scales
 
-        def quantise_w1(a, b, on_vector, pieces=((0, PASS),)):
-            grouped = ring.tile([P, PACK * PASS], BF16, name="w1_bf", tag="w1_bf%d%d" % (a, b), bufs=1, align_bytes=64)
-            dst = grouped[:].rearrange("p (t m j) -> p m j t", t=PACK, j=PACK)
-            src = w1_raw[a, b].rearrange("p j (m t) -> p m j t", t=PACK)
+        def quantise_w1(a, b, first, last, on_vector):
+            if (a, b) not in w1q_w:
+                w1q_w[a, b] = kept("w1q_w%d%d" % (a, b), [P, PASS], U32)
+                w1q_s[a, b] = kept("w1q_s%d%d" % (a, b), [P, PASS], U8)
+            grouped = kept("w1_bf%d%d%d" % (a, b, first), [P, PACK * P * (last - first)], BF16)
+            dst = grouped[:].rearrange("p (t m j) -> p m j t", m=P, j=PACK)
+            src = w1_raw[a, b].rearrange("p j (m t) -> p m j t", t=PACK)[:, :, :, first:last]
             if on_vector:
                 nc.vector.tensor_scalar(dst, src, -2.0, None, ALU.mult)
             else:
                 nc.scalar.activation(dst, src, ACT.Copy, scale=-2.0)
-            words = kept("w1q_w%d%d" % (a, b), [P, PASS], U32)
-            scales = kept("w1q_s%d%d" % (a, b), [P, PASS], U8)
-            for first, last in pieces:
-                nc.vector.quantize_mx(
-                    out=words[:, first:last].bitcast(FP8X4),
-                    scales=scales[:, first:last],
-                    in_=grouped[:, PACK * first : PACK * last],
-                )
-            w1q_w[a, b], w1q_s[a, b] = words, scales
+            cols = slice(first * P, last * P)
+            nc.vector.quantize_mx(out=w1q_w[a, b][:, cols].bitcast(FP8X4), scales=w1q_s[a, b][:, cols], in_=grouped[:])
             w1_rounded[a, b] = grouped
 
         sin_sq = {}
 
         def angle_part(b, t, reuse=None):
-            angle = psum.tile([P, S], F32, name="angle", tag="angle", bufs=4)
+            angle = psum.tile([P, S], F32, name="angle", tag="angle", bufs=2)
             for a in range(2):
                 nc.tensor.matmul_mx(
                     out=angle[:],
@@ -193,7 +189,7 @@ def tile_list_tree_ring_matching_kernel(
 
         def feature(b, t, reuse=None):
             cols = slice(t * P, (t + 1) * P)
-            amp = psum.tile([P, S], F32, name="amp", tag="amp", bufs=4)
+            amp = psum.tile([P, S], F32, name="amp", tag="amp", bufs=6)
             passes = (0, 1) if t == 0 else (1, 0)
             for a in passes:
                 nc.tensor.matmul_mx(
@@ -300,20 +296,19 @@ def tile_list_tree_ring_matching_kernel(
                         in_=last_x[u][:].rearrange("p j t -> p (j t)"),
                     )
 
+        def weave_page(c):
+            weave(nc.scalar.copy, first_woven[c][:], page_planes[:, :, c * PAGE_CHUNK : (c + 1) * PAGE_CHUNK])
+
         def quantise_page(b, c):
-            if b == 0:
-                woven = first_woven[c]
-                weave(nc.scalar.copy, woven[:], page_planes[:, :, c * PAGE_CHUNK : (c + 1) * PAGE_CHUNK])
-                rounded = woven[:]
-            else:
-                rounded = last_woven[c][:].rearrange("p m t -> p (m t)")
+            rounded = first_woven[c][:] if b == 0 else last_woven[c][:].rearrange("p m t -> p (m t)")
             nc.vector.quantize_mx(out=page_w[b][c][:].bitcast(FP8X4), scales=page_s[b][c][:], in_=rounded)
 
         scores = {}
 
         def score_pass(b, mt):
             if b == 0:
-                scores[mt] = psum.tile([P, NP], F32, name="score", tag="angle" if mt < 4 else "amp", bufs=4)
+                tag, bufs = ("angle", 2) if mt < 2 else ("amp", 6)
+                scores[mt] = psum.tile([P, NP], F32, name="score", tag=tag, bufs=bufs)
             c, first = divmod(mt * P, PAGE_CHUNK)
             cols = slice(first, first + P)
             nc.tensor.matmul_mx(
@@ -326,20 +321,23 @@ def tile_list_tree_ring_matching_kernel(
                 stop=(b == 1),
             )
 
-        def finish(mt):
+        def finish(mt, parts):
             sig = ring.tile([P, NP], F32, name="sig", tag="act", bufs=4)
-            nc.scalar.activation(sig[:], scores[mt][:], ACT.Sigmoid)
             res = ring.tile([P, NP], F32, name="res", tag="sin_sq", bufs=8)
-            nc.vector.tensor_tensor(res[:], sig[:], gm_sb[mt // PACK][:, mt % PACK, :], ALU.mult)
-            nc.sync.dma_start(out=out[mt * P : (mt + 1) * P, :], in_=res[:])
+            for u in range(parts):
+                cols = slice(u * NP // parts, (u + 1) * NP // parts)
+                nc.scalar.activation(sig[:, cols], scores[mt][:, cols], ACT.Sigmoid)
+                nc.vector.tensor_tensor(res[:, cols], sig[:, cols], gm_sb[mt // PACK][:, mt % PACK, cols], ALU.mult)
+                nc.sync.dma_start(out=out[mt * P : (mt + 1) * P, cols], in_=res[:, cols])
 
         deal_w4(0, nc.vector.tensor_copy)
-        quantise_w1(0, 0, True)
+        quantise_w1(0, 0, 0, PACK, True)
         angle_part(0, 0)
-        quantise_w1(1, 0, True, ((0, P), (P, PASS)))
+        quantise_w1(1, 0, 0, 1, True)
         feature(0, 0)
+        quantise_w1(1, 0, 1, PACK, False)
         for t in range(1, PACK):
-            angle_part(0, t)
+            angle_part(0, t, w1_raw[1, 0][:, t, :])
         place(0, 0)
         pick(0, 0)
         feature(0, 1, features[0, 0])
@@ -348,8 +346,8 @@ def tile_list_tree_ring_matching_kernel(
         feature(0, 2, features[0, 0])
         pick(0, 1)
         clip(0, 1, nc.vector)
-        quantise_w1(0, 1, False)
-        quantise_w1(1, 1, False)
+        quantise_w1(0, 1, 0, PACK, False)
+        quantise_w1(1, 1, 0, PACK, False)
         deal_w4(1, nc.scalar.copy)
         angle_part(1, 0)
         angle_part(1, 1)
@@ -376,13 +374,16 @@ def tile_list_tree_ring_matching_kernel(
         pick(1, 1)
         clip(1, 1, nc.vector)
         for c in range(chunks):
-            quantise_page(0, c)
+            weave_page(c)
         round_x(0, 3)
-        quantise_x(0)
+        quantise_page(0, 0)
         place(1, 2)
         feature(1, 3, features[1, 1])
         pick(1, 2)
         clip(1, 2, nc.vector)
+        for c in range(1, chunks):
+            quantise_page(0, c)
+        quantise_x(0)
         for mt in range(T2 // P):
             score_pass(0, mt)
         round_page(1, 0)
@@ -408,4 +409,4 @@ def tile_list_tree_ring_matching_kernel(
                 quantise_page(1, c)
             for mt in range(c * PAGE_CHUNK // P, (c + 1) * PAGE_CHUNK // P):
                 score_pass(1, mt)
-                finish(mt)
+                finish(mt, 2 if mt == T2 // P - 1 else 1)

from contextlib import ExitStack

import concourse.mybir as mybir

K, T, S, H, T2, NP = 1024, 2048, 512, 1024, 1024, 512
FLOPS = 2 * K * H * S * 2 + 2 * H * T2 * NP

F32 = mybir.dt.float32
BF16 = mybir.dt.bfloat16
I32 = mybir.dt.int32
U32 = mybir.dt.uint32
U16 = mybir.dt.uint16
U8 = mybir.dt.uint8
FP8X4 = mybir.dt.float8_e4m3fn_x4
FP4X4 = mybir.dt.float4_e2m1fn_x4
ALU = mybir.AluOpType
ACT = mybir.ActivationFunctionType

P = 128
PACK = 4
PASS = P * PACK
PAGE_CHUNK = 256


def tile_list_tree_ring_matching_kernel(
    tc, tab_words, tab_scales, offs, offs2, offs3, w1, w4_words, w4_scales, wgs, page0, lo, hi, gain, gm, out
):
    nc = tc.nc
    with ExitStack() as ctx:
        lists = ctx.enter_context(tc.tile_pool(name="lists", bufs=1))
        keep = ctx.enter_context(tc.tile_pool(name="keep", bufs=1))
        ring = ctx.enter_context(tc.tile_pool(name="ring", bufs=2))
        psum = ctx.enter_context(tc.psum_pool(name="psum", bufs=1))

        def kept(name, shape, dtype):
            return keep.tile(shape, dtype, name=name, align_bytes=64)

        idx = lists.tile([P, S // 16], U16, name="idx")
        idx2 = lists.tile([P, S // 16], U16, name="idx2")
        idx3 = lists.tile([P, NP // 16], U16, name="idx3")

        tab_w = [kept("tab_w%d" % a, [P, T], I32) for a in range(2)]
        tab_s = kept("tab_s", [P, 2, T], U8)
        w4_w = [kept("w4_w%d" % b, [P, 2, 2 * PASS], U8) for b in range(2)]
        w4_s = [kept("w4_s%d" % b, [P, 2, PASS], U8) for b in range(2)]
        wgs_sb = kept("wgs_sb", [P, PACK, S], F32)
        page = [[kept("page%d%d" % (b, t), [P, T2], F32) for t in range(PACK)] for b in range(2)]
        lo_sb = kept("lo_sb", [P, 2, PACK], F32)
        hi_sb = kept("hi_sb", [P, 2, PACK], F32)
        gain_sb = kept("gain_sb", [P, 2, PACK], F32)

        nc.vector.memset(tab_s[:].rearrange("p a t -> p (a t)").bitcast(I32), 0)
        for b in range(2):
            nc.gpsimd.memset(w4_s[b][:].rearrange("p a t -> p (a t)").bitcast(I32), 0)

        w1_raw = {}

        stage = kept("stage", [P, 9 * PASS], F32)

        def load_w1(a, b):
            if b == 0:
                raw = ring.tile([P, PACK, PASS], F32, name="w1_raw", tag="big", bufs=2, align_bytes=64)[:]
            else:
                raw = stage[:, a * PACK * PASS : (a + 1) * PACK * PASS].rearrange("p (j c) -> p j c", j=PACK)
            rows = w1[a * PASS : (a + 1) * PASS, b * PASS : (b + 1) * PASS].rearrange("(p j) c -> p j c", j=PACK)
            nc.sync.dma_start(out=raw, in_=rows)
            w1_raw[a, b] = raw

        def load_w4(b):
            src = w4_words.rearrange("a p c -> p a c")[:, :, 2 * PASS * b : 2 * PASS * (b + 1)]
            nc.sync.dma_start(out=w4_w[b][:].bitcast(I32), in_=src.bitcast(I32))

        def load_page(b, t):
            rows = page0[b * PASS : (b + 1) * PASS, :].rearrange("(p t) m -> p t m", t=PACK)
            nc.sync.dma_start(out=page[b][t][:], in_=rows[:, t, :])

        def load_scale_rows(dst, src):
            rows = src.rearrange("a q c -> q a c")
            for quad in range(4):
                nc.sync.dma_start(
                    out=dst[32 * quad : 32 * quad + 4, :, :].bitcast(I32),
                    in_=rows[4 * quad : 4 * quad + 4, :, :].bitcast(I32),
                )

        def load_wgs(first, last):
            for quad in (0, 2, 1, 3):
                nc.sync.dma_start(
                    out=wgs_sb[32 * quad : 32 * quad + 32, first:last, :],
                    in_=wgs.rearrange("(p t) j -> p t j", t=PACK)[:, first:last, :],
                )

        def load_table(a):
            nc.sync.dma_start(out=tab_w[a][:], in_=tab_words[a].rearrange("p t i -> p (t i)").bitcast(I32))

        nc.sync.dma_start(idx[:], offs)
        load_table(0)
        load_scale_rows(tab_s, tab_scales)
        load_table(1)
        load_w4(0)
        load_scale_rows(w4_s[0], w4_scales[:, :, :PASS])
        load_w1(0, 0)
        load_w1(1, 0)
        load_page(0, 0)
        nc.sync.dma_start(idx2[:], offs2)
        load_wgs(0, 1)
        load_page(0, 1)
        nc.sync.dma_start(idx3[:], offs3)
        load_wgs(1, 2)
        load_w1(0, 1)
        for dst, src in ((lo_sb, lo), (hi_sb, hi), (gain_sb, gain)):
            nc.sync.dma_start(out=dst[:], in_=src.rearrange("(b p t) -> p b t", b=2, t=PACK))
        load_w1(1, 1)
        load_w4(1)
        load_page(0, 2)
        load_scale_rows(w4_s[1], w4_scales[:, :, PASS:])
        load_page(0, 3)
        load_wgs(2, 3)
        load_page(1, 0)
        load_page(1, 1)
        load_page(1, 2)
        load_wgs(3, 4)
        gm_sb = []
        for half in range(2):
            g = ring.tile([P, PACK, NP], F32, name="gm_sb", tag="big", bufs=2, align_bytes=64)
            rows = gm[half * PASS : (half + 1) * PASS, :]
            nc.sync.dma_start(out=g[:], in_=rows.rearrange("(c p) j -> p c j", p=P))
            gm_sb.append(g)
        load_page(1, 3)

        v_w = [kept("v_w%d" % a, [P, S], U32) for a in range(2)]
        v_s = [kept("v_s%d" % a, [P, S], U8) for a in range(2)]
        for a in range(2):
            nc.vector.tensor_copy(v_w[a][:], tab_w[a][:].bitcast(U32).indirect(idx[:]))
            nc.vector.tensor_copy(v_s[a][:], tab_s[:, a, :].indirect(idx[:]))

        w4p_w, w4p_s, w1q_w, w1q_s, w1_rounded = {}, {}, {}, {}, {}

        def deal_w4(b, copy_words):
            words = kept("w4p_w%d" % b, [P, 2, 2 * PASS], U8)
            scales = kept("w4p_s%d" % b, [P, 2, PASS], U8)
            copy_words(
                words[:].bitcast(U16).rearrange("p a (t m) -> p a t m", t=PACK),
                w4_w[b][:].bitcast(U16).rearrange("p a (m t) -> p a t m", t=PACK),
            )
            nc.vector.tensor_copy(
                scales[:].rearrange("p a (t m) -> p a t m", t=PACK),
                w4_s[b][:].rearrange("p a (m t) -> p a t m", t=PACK),
            )
            w4p_w[b], w4p_s[b] = words, scales

        def quantise_w1(a, b, first, last, on_vector):
            if (a, b) not in w1q_w:
                w1q_w[a, b] = kept("w1q_w%d%d" % (a, b), [P, PASS], U32)
                w1q_s[a, b] = kept("w1q_s%d%d" % (a, b), [P, PASS], U8)
            grouped = kept("w1_bf%d%d%d" % (a, b, first), [P, PACK * P * (last - first)], BF16)
            dst = grouped[:].rearrange("p (t m j) -> p m j t", m=P, j=PACK)
            src = w1_raw[a, b].rearrange("p j (m t) -> p m j t", t=PACK)[:, :, :, first:last]
            if on_vector:
                nc.vector.tensor_scalar(dst, src, -2.0, None, ALU.mult)
            else:
                nc.scalar.activation(dst, src, ACT.Copy, scale=-2.0)
            cols = slice(first * P, last * P)
            nc.vector.quantize_mx(out=w1q_w[a, b][:, cols].bitcast(FP8X4), scales=w1q_s[a, b][:, cols], in_=grouped[:])
            w1_rounded[a, b] = grouped

        sin_sq = {}

        def angle_part(b, t, reuse=None):
            angle = psum.tile([P, S], F32, name="angle", tag="angle", bufs=2)
            for a in range(2):
                nc.tensor.matmul_mx(
                    out=angle[:],
                    lhsT=w4p_w[b][:, a, 2 * t * P : 2 * (t + 1) * P].bitcast(FP4X4),
                    lhsT_scale=w4p_s[b][:, a, t * P : (t + 1) * P],
                    rhs=v_w[a][:].bitcast(FP8X4),
                    rhs_scale=v_s[a][:],
                    start=(a == 0),
                    stop=(a == 1),
                )
            if reuse is None:
                sin_half = ring.tile([P, S], F32, name="sin_half", tag="act", bufs=4)[:]
            else:
                sin_half = reuse
            nc.scalar.activation(sin_half, angle[:], ACT.Sin, scale=0.5)
            sin_sq[b, t] = ring.tile([P, S], F32, name="sin_sq", tag="sin_sq", bufs=8)
            nc.scalar.activation(sin_sq[b, t][:], sin_half, ACT.Square)

        features = {}

        def feature(b, t, reuse=None):
            cols = slice(t * P, (t + 1) * P)
            amp = psum.tile([P, S], F32, name="amp", tag="amp", bufs=6)
            passes = (0, 1) if t == 0 else (1, 0)
            for a in passes:
                nc.tensor.matmul_mx(
                    out=amp[:],
                    lhsT=w1q_w[a, b][:, cols].bitcast(FP8X4),
                    lhsT_scale=w1q_s[a, b][:, cols],
                    rhs=v_w[a][:].bitcast(FP8X4),
                    rhs_scale=v_s[a][:],
                    start=(a == passes[0]),
                    stop=(a == passes[1]),
                )
            if reuse is None:
                h = ring.tile([P, S], F32, name="h", tag="h", bufs=1, align_bytes=64)[:]
            else:
                h = reuse
            nc.vector.scalar_tensor_tensor(h, sin_sq[b, t][:], 0.5, amp[:], ALU.subtract, ALU.mult)
            features[b, t] = h

        page_planes = stage[:, 3 * PASS : 7 * PASS].bitcast(BF16).rearrange("p (t m) -> p t m", t=PACK)
        x_planes = stage[:, 7 * PASS :].bitcast(BF16).rearrange("p (t m) -> p t m", t=PACK)
        chunks = T2 // PAGE_CHUNK
        first_woven = [kept("first_woven%d" % c, [P, PACK * PAGE_CHUNK], BF16) for c in range(chunks)]
        last_woven = [kept("last_woven%d" % c, [P, PAGE_CHUNK, PACK], BF16) for c in range(chunks)]
        first_x = kept("first_x", [P, PACK * NP], BF16)
        last_x = [kept("last_x%d" % u, [P, NP // 2, PACK], BF16) for u in range(2)]
        last_planes = kept("last_planes", [P, 2, T2], BF16)
        last_x_planes = kept("last_x_planes", [P, 2, NP], BF16)
        picked, clipped = {}, {}

        def place(b, t):
            nc.vector.tensor_tensor(
                page[b][t][:].indirect(idx2[:]), features[b, t], wgs_sb[:, t, :], ALU.mult
            )

        def pick(b, t, parts=1):
            picked[b, t] = ring.tile([P, NP], F32, name="picked", bufs=4)
            width = NP // parts
            for u in range(parts):
                entries = idx3[:, u * width // 16 : (u + 1) * width // 16]
                nc.vector.tensor_copy(picked[b, t][:, u * width : (u + 1) * width], page[b][t][:].indirect(entries))

        def clip(b, t, engine, parts=1, reuse=None):
            if reuse is None:
                clipped[b, t] = ring.tile([P, NP], F32, name="clipped", bufs=4)[:]
            else:
                clipped[b, t] = reuse
            width = NP // parts
            for u in range(parts):
                cols = slice(u * width, (u + 1) * width)
                engine.tensor_scalar(
                    clipped[b, t][:, cols],
                    picked[b, t][:, cols],
                    hi_sb[:, b, t : t + 1],
                    lo_sb[:, b, t : t + 1],
                    ALU.min,
                    ALU.max,
                )

        def round_page(b, t):
            if t < (PACK - 1 if b == 0 else 2):
                nc.scalar.copy((page_planes if b == 0 else last_planes)[:, t, :], page[b][t][:])
                return
            for c in range(chunks):
                cols = slice(c * PAGE_CHUNK, (c + 1) * PAGE_CHUNK)
                nc.scalar.copy(page_planes[:, t, cols] if b == 0 else last_woven[c][:, :, t], page[b][t][:, cols])

        def round_x(b, t):
            factor = gain_sb[:, b, t : t + 1]
            if b == 0 or t < 2:
                planes = x_planes if b == 0 else last_x_planes
                nc.scalar.activation(planes[:, t, :], clipped[b, t], ACT.Copy, scale=factor)
                return
            for u in range(2):
                src = clipped[b, t][:, u * NP // 2 : (u + 1) * NP // 2]
                if t == 2:
                    nc.scalar.activation(last_x[u][:, :, t], src, ACT.Copy, scale=factor)
                else:
                    nc.vector.tensor_scalar(last_x[u][:, :, t], src, factor, None, ALU.mult)

        def weave_pair(dst, src):
            nc.scalar.copy(
                dst[:, :, :2].rearrange("p (c i) t -> p c t i", i=4), src.rearrange("p t (c i) -> p c t i", i=4)
            )

        x_w = [kept("x_w%d" % b, [P, NP], U32) for b in range(2)]
        x_s = [kept("x_s%d" % b, [P, NP], U8) for b in range(2)]
        page_w = [[kept("page_w%d%d" % (b, c), [P, PAGE_CHUNK], U32) for c in range(chunks)] for b in range(2)]
        page_s = [[kept("page_s%d%d" % (b, c), [P, PAGE_CHUNK], U8) for c in range(chunks)] for b in range(2)]

        def weave(copy, dst, src):
            copy(dst.rearrange("p (c i t) -> p c t i", i=4, t=PACK), src.rearrange("p t (c i) -> p c t i", i=4))

        def quantise_x(b):
            if b == 0:
                woven = first_x
                weave(nc.scalar.copy, woven[:], x_planes)
                nc.vector.quantize_mx(out=x_w[b][:].bitcast(FP8X4), scales=x_s[b][:], in_=woven[:])
            else:
                for u in range(2):
                    cols = slice(u * NP // 2, (u + 1) * NP // 2)
                    nc.vector.quantize_mx(
                        out=x_w[b][:, cols].bitcast(FP8X4),
                        scales=x_s[b][:, cols],
                        in_=last_x[u][:].rearrange("p j t -> p (j t)"),
                    )

        def weave_page(c):
            weave(nc.scalar.copy, first_woven[c][:], page_planes[:, :, c * PAGE_CHUNK : (c + 1) * PAGE_CHUNK])

        def quantise_page(b, c):
            rounded = first_woven[c][:] if b == 0 else last_woven[c][:].rearrange("p m t -> p (m t)")
            nc.vector.quantize_mx(out=page_w[b][c][:].bitcast(FP8X4), scales=page_s[b][c][:], in_=rounded)

        scores = {}

        def score_pass(b, mt):
            if b == 0:
                tag, bufs = ("angle", 2) if mt < 2 else ("amp", 6)
                scores[mt] = psum.tile([P, NP], F32, name="score", tag=tag, bufs=bufs)
            c, first = divmod(mt * P, PAGE_CHUNK)
            cols = slice(first, first + P)
            nc.tensor.matmul_mx(
                out=scores[mt][:],
                lhsT=page_w[b][c][:, cols].bitcast(FP8X4),
                lhsT_scale=page_s[b][c][:, cols],
                rhs=x_w[b][:].bitcast(FP8X4),
                rhs_scale=x_s[b][:],
                start=(b == 0),
                stop=(b == 1),
            )

        def finish(mt, parts):
            sig = ring.tile([P, NP], F32, name="sig", tag="act", bufs=4)
            res = ring.tile([P, NP], F32, name="res", tag="sin_sq", bufs=8)
            for u in range(parts):
                cols = slice(u * NP // parts, (u + 1) * NP // parts)
                nc.scalar.activation(sig[:, cols], scores[mt][:, cols], ACT.Sigmoid)
                nc.vector.tensor_tensor(res[:, cols], sig[:, cols], gm_sb[mt // PACK][:, mt % PACK, cols], ALU.mult)
                nc.sync.dma_start(out=out[mt * P : (mt + 1) * P, cols], in_=res[:, cols])

        deal_w4(0, nc.vector.tensor_copy)
        quantise_w1(0, 0, 0, PACK, True)
        angle_part(0, 0)
        quantise_w1(1, 0, 0, 1, True)
        feature(0, 0)
        quantise_w1(1, 0, 1, PACK, False)
        for t in range(1, PACK):
            angle_part(0, t, w1_raw[1, 0][:, t, :])
        place(0, 0)
        pick(0, 0)
        feature(0, 1, features[0, 0])
        place(0, 1)
        clip(0, 0, nc.vector)
        feature(0, 2, features[0, 0])
        pick(0, 1)
        clip(0, 1, nc.vector)
        quantise_w1(0, 1, 0, PACK, False)
        quantise_w1(1, 1, 0, PACK, False)
        deal_w4(1, nc.scalar.copy)
        angle_part(1, 0)
        angle_part(1, 1)
        angle_part(1, 2, stage[:, 6 * PASS : 7 * PASS])
        angle_part(1, 3, stage[:, 8 * PASS :])
        place(0, 2)
        feature(0, 3, w1_rounded[1, 1][:].bitcast(F32)[:, :S])
        pick(0, 2)
        place(0, 3)
        clip(0, 2, nc.vector)
        pick(0, 3)
        feature(1, 0, features[0, 3])
        clip(0, 3, nc.vector)
        place(1, 0)
        feature(1, 1, picked[0, 3][:])
        for t in range(PACK - 1):
            round_page(0, t)
            round_x(0, t)
        round_page(0, 3)
        pick(1, 0)
        place(1, 1)
        clip(1, 0, nc.vector)
        feature(1, 2, features[1, 0])
        pick(1, 1)
        clip(1, 1, nc.vector)
        for c in range(chunks):
            weave_page(c)
        round_x(0, 3)
        quantise_page(0, 0)
        place(1, 2)
        feature(1, 3, features[1, 1])
        pick(1, 2)
        clip(1, 2, nc.vector)
        for c in range(1, chunks):
            quantise_page(0, c)
        quantise_x(0)
        for mt in range(T2 // P):
            score_pass(0, mt)
        round_page(1, 0)
        round_page(1, 1)
        round_x(1, 0)
        for c in range(chunks):
            if c == chunks - 1:
                round_x(1, 1)
            weave_pair(last_woven[c], last_planes[:, :, c * PAGE_CHUNK : (c + 1) * PAGE_CHUNK])
        for u in range(2):
            weave_pair(last_x[u], last_x_planes[:, :, u * NP // 2 : (u + 1) * NP // 2])
        round_page(1, 2)
        round_x(1, 2)
        place(1, 3)
        round_page(1, 3)
        pick(1, 3, 2)
        clip(1, 3, nc.vector, 2, clipped[1, 2])
        round_x(1, 3)
        quantise_page(1, 0)
        quantise_x(1)
        for c in range(chunks):
            if c > 0:
                quantise_page(1, c)
            for mt in range(c * PAGE_CHUNK // P, (c + 1) * PAGE_CHUNK // P):
                score_pass(1, mt)
                finish(mt, 2 if mt == T2 // P - 1 else 1)
